import numpy as np, ml_dtypes
CORES = [2,3,42,43,82,83,122,123]
N = 8
import mx_ref
NC, G = 128, 4
C, C2 = np.float32(0.043), np.float32(0.0152)
BF = ml_dtypes.bfloat16
def cut(t, i, w=512):
    return t[:, w * i:w * i + w]
def tile(rs):
    return np.stack(rs, axis=2).reshape(128, -1).astype(BF)
def layer(w, X):
    out = []
    for i in range(G):
        for t in range(len(X)):
            p = mx_ref.matmul(mx_ref.quantize(cut(w, len(X) * i + t)), X[t])
            z = p if t == 0 else z + p
        out.append(z)
    return out
def act(Z):
    return [np.maximum(z, 0) * C for z in Z]
def act2(Z):
    return [np.maximum(z, 0) * C2 for z in Z]
def setup_inputs(rng):
    def f(*shape):
        return mx_ref.flush((rng.standard_normal(shape, dtype=np.float32) * np.exp2(rng.integers(-2, 3, shape[:-1] + (1,)))).astype(BF))
    return {"x": f(N, 128, 4 * NC), "w1": f(N, 128, G * 512), "w2": f(N, 128, G * 512), "w3": f(N, 128, G * 512), "w4": f(N, 128, 512)}
def setup_inputs_blocks(rng):
    d = setup_inputs(rng)
    for k in ("x", "w1", "w2", "w3", "w4"): d[k] = mx_ref.spread(d[k], rng, 2)
    return d
def setup_inputs_wide(rng):
    d = setup_inputs(rng)
    for k in ("x", "w1", "w2", "w3", "w4"): d[k] = mx_ref.flush((d[k].astype(np.float32) * np.exp2(rng.integers(-4, 5, (N, 1, 1))).astype(np.float32)).astype(BF))
    return d
def reference(x, w1, w2, w3, w4, own=None):
    X = [mx_ref.quantize(x[j]) for j in range(N)]
    t = np.stack([np.stack([tile(act(layer(w1[r], [X[c]]))) for c in range(N)]) for r in range(N)])
    uset = t if own is None else own["t"]
    h = np.zeros((N, 128, 4 * NC), BF)
    for c in range(N):
        for r in range(N):
            P = layer(w2[r], [mx_ref.quantize(uset[r][c])])
            Z = P if r == 0 else [z + p for z, p in zip(Z, P)]
        h[c] = tile(act2(Z))
    use = h if own is None else own["h"]
    H = [mx_ref.quantize(use[j]) for j in range(N)]
    y = np.zeros((N, 128, NC), np.float32)
    for c in range(N):
        for r in range(N):
            p = mx_ref.matmul(mx_ref.quantize(w4[r]), mx_ref.quantize(tile(act(layer(w3[r], [H[c]])))))
            y[c] = p if r == 0 else y[c] + p
    return {"t": t, "h": h, "y": y}

@@ -1,0 +1,325 @@
+import numpy as np
+from concourse.bass import DstId, RemoteDMATransfer
+from concourse.mybir import dt, AluOpType, ActivationFunctionType
+
+F8, U8, BF, F32 = "float8_e4m3fn_x4", "uint8", "bfloat16", "float32"
+SCRATCH = {
+    "xt": ("sbuf", [128, 512], BF), "w1t": ("sbuf", [128, 2048], BF), "w2t": ("sbuf", [128, 2048], BF),
+    "w3t": ("sbuf", [128, 2048], BF), "w4t": ("sbuf", [128, 512], BF),
+    "xc": ("sbuf", [128, 1024], F8), "xp": ("sbuf", [128, 1024], U8),
+    "w1c": ("sbuf", [128, 512], F8), "w1p": ("sbuf", [128, 512], U8),
+    "w2c": ("sbuf", [128, 1024], F8), "w2p": ("sbuf", [128, 1024], U8),
+    "w34c": ("sbuf", [128, 1280], F8), "w34p": ("sbuf", [128, 1280], U8),
+    "tt": ("sbuf", [128, 4096], BF), "tc": ("sbuf", [128, 1024], F8), "tp": ("sbuf", [128, 1024], U8),
+    "rc": ("sbuf", [128, 512], F8), "rp": ("sbuf", [128, 512], U8),
+    "so": ("sbuf", [128, 1536], F32), "si": ("sbuf", [128, 1536], F32), "sacc": ("sbuf", [128, 512], F32),
+    "ht": ("sbuf", [128, 512], BF), "hc": ("sbuf", [128, 512], F8), "hp": ("sbuf", [128, 512], U8),
+    "ut": ("sbuf", [128, 4096], BF), "uc": ("sbuf", [128, 1024], F8), "up": ("sbuf", [128, 1024], U8),
+    "yo": ("sbuf", [128, 384], F32), "yi": ("sbuf", [128, 384], F32), "ya": ("sbuf", [128, 128], F32),
+    "rl": ("sbuf", [128, 768], F32),
+}
+for _b in range(8):
+    SCRATCH["z%d" % _b] = ("psum", [128, 512], F32)
+SEMAPHORES = (["xa%d" % c for c in range(8)] + ["xb%d" % c for c in range(8)] + ["w2s", "w34s", "ts0", "ts1"]
+              + ["%s%d" % (n, s) for n in ("sd", "sh", "rs", "ys") for s in (1, 2, 3)] + ["hs%d" % k for k in range(4)]
+              + ["lx", "lw1", "lw2", "lw3", "lw4", "st", "te", "ve", "ac", "gate", "sent", "ssent", "hsent"])
+C1, C2 = float(np.float32(0.043)), float(np.float32(0.0152))
+ADD, MAX, MUL = AluOpType.add, AluOpType.max, AluOpType.mult
+RELU, COPY = ActivationFunctionType.Relu, ActivationFunctionType.Copy
+
+
+def _layout(T, topo):
+    chips = []
+    for c in T.cores:
+        if topo.chip(c) not in chips:
+            chips.append(topo.chip(c))
+    ranks = [[r for r, c in enumerate(T.cores) if topo.chip(c) == ch] for ch in chips]
+    relays = []
+    for ch, rs in zip(chips, ranks):
+        own = T.cores[rs[0]]
+        near = [c for c in range(128) if topo.chip(c) == ch and topo.die(c) != topo.die(own)]
+        relays.append([c for c in near if all(topo.may_write(c, d) for d in T.cores)][:len(rs)])
+    return chips, ranks, relays
+
+
+def _tools(g, T, topo):
+    queues = {"g": g, "te": g.tensor, "ve": g.vector, "ac": g.scalar, "sy": g.sync}
+    seen, local = {}, {}
+
+    def wait(q, sem, n):
+        if n > seen.get((q, sem), 0):
+            seen[(q, sem)] = n
+            queues[q].wait_ge(T.sem[sem], n)
+
+    def dest(c):
+        rid, pid, _ = topo.addr(c)
+        return DstId(rid=rid, pnc=pid)
+
+    def part(mask, sem, src, outs):
+        return RemoteDMATransfer(dst_ids=[dest(c) for c, _ in outs], dma_engine_mask=mask, remote_sem=T.sem[sem],
+                                 srcs=[src], dsts=[o for _, o in outs])
+
+    def send(parts, masks, sem="sent"):
+        g.remote_dma_fused(parts, local_sem=T.sem[sem])
+        local[sem] = local.get(sem, 0) + sum(bin(m).count("1") for m in masks)
+
+    return wait, part, send, local
+
+
+def _codes(buf, a, b):
+    return buf[:, a:b].bitcast(dt.uint8)
+
+
+def _relay(g, T, topo, core, r, opp):
+    wait, part, send, local = _tools(g, T, topo)
+    a, b = 128 * r, 128 * r + 128
+    off = topo.mask(core, opp[0][1])
+    wait("g", "xa%d" % r, 8)
+    send([part(off, "xa%d" % r, _codes(T.xc, a, b), [(c, _codes(T.xc, a, b)) for _, c in opp])], [off])
+    wait("g", "xb%d" % r, 8)
+    send([part(off, "xb%d" % r, T.xp[:, a:b], [(c, T.xp[:, a:b]) for _, c in opp])], [off])
+    for i, (s, c) in enumerate(opp):
+        wait("g", "rs%d" % s, 8)
+        send([part(off, "sh%d" % s, T.rl[:, 256 * i:256 * i + 256],
+                   [(c, T.si[:, 512 * (s - 1) + 256:512 * s])])], [off])
+    wait("g", "sent", local["sent"])
+
+
+def rank_program(g, core, T, topo):
+    chips, ranks, relays = _layout(T, topo)
+    if topo.chip(core) not in chips:
+        return
+    k = chips.index(topo.chip(core))
+    steps = sorted((1, 2, 3), key=lambda s: (not topo.same_plane(chips[k], chips[k ^ s]), s))
+    if core in relays[k]:
+        j = relays[k].index(core)
+        return _relay(g, T, topo, core, ranks[k][j], [(s, T.cores[ranks[k ^ s][1 - j]]) for s in steps])
+    r = T.rank_of(core)
+    if r is None:
+        return
+    j = ranks[k].index(r)
+    p = ranks[k][1 - j]
+    pc, rl = T.cores[p], relays[k][j]
+    same = [ranks[k ^ s][j] for s in steps]
+    opp = [ranks[k ^ s][1 - j] for s in steps]
+    wait, part, send, local = _tools(g, T, topo)
+    sem = T.sem
+    on, off = topo.mask(core, pc), topo.mask(core, T.cores[same[0]])
+    rest = on & ~off
+    te, ve, ac, sy = g.tensor, g.vector, g.scalar, g.sync
+    n = {"te": 0, "ve": 0, "ac": 0}
+
+    def done(call, q):
+        call.then_inc(sem[q], 1)
+        n[q] += 1
+        return n[q]
+
+    sy.dma_start(T.xt[:], T.x[:]).then_inc(sem.lx, 16)
+    sy.dma_start(T.w1t[:], T.w1[:]).then_inc(sem.lw1, 16)
+    wait("sy", "gate", 1)
+    sy.dma_start(T.w2t[:], T.w2[:]).then_inc(sem.lw2, 16)
+    sy.dma_start(T.w3t[:], T.w3[:]).then_inc(sem.lw3, 16)
+    sy.dma_start(T.w4t[:], T.w4[:]).then_inc(sem.lw4, 16)
+
+    def quant(codes, plane, a, src, b, w):
+        return done(ve.quantize_mx(codes[:, a:a + w], plane[:, a:a + w], src[:, b:b + 4 * w]), "ve")
+
+    banks = [T["z%d" % b] for b in range(8)]
+    free, turn = [None] * 8, [0]
+
+    def product(terms):
+        b = turn[0]
+        turn[0] = (b + 1) % 8
+        if free[b]:
+            wait("te", *free[b])
+        for i, (wc, wp, a, xc, xp, c) in enumerate(terms):
+            call = te.matmul_mx(banks[b][:, 0:128], wc[:, a:a + 128], wp[:, a:a + 128], xc[:, c:c + 128],
+                                xp[:, c:c + 128], i == 0, i == len(terms) - 1)
+        return b, done(call, "te")
+
+    def empty(q, res, out, scale=None):
+        b, m = res
+        wait(q, "te", m)
+        z = banks[b][:, 0:128]
+        if q == "ac":
+            call = ac.activation(out, z, COPY) if scale is None else ac.activation(out, z, RELU, scale=scale)
+        else:
+            call = ve.tensor_copy(out, z) if scale is None else ve.tensor_scalar(out, z, 0.0, scale, MAX, MUL)
+        free[b] = (q, done(call, q))
+        return free[b]
+
+    def layer(wc, wp, a, xc, xp, c, tile, codes, plane, pos):
+        res = [product([(wc, wp, a + 128 * i, xc, xp, c)]) for i in range(4)]
+        ends = [empty("ac" if i % 2 == 0 else "ve", res[i], tile[:, 512 * pos + i:512 * pos + 512:4], C1)
+                for i in range(4)]
+        for e in ends[2:]:
+            wait("ve", *e)
+        return quant(codes, plane, 128 * pos, tile, 512 * pos, 128), ends
+
+    wait("ve", "lx", 16)
+    x_ready = quant(T.xc, T.xp, 128 * r, T.xt, 0, 128)
+    a, b = 128 * r, 128 * r + 128
+    wait("g", "ve", x_ready)
+    for name, v in (("xa%d" % r, _codes(T.xc, a, b)), ("xb%d" % r, T.xp[:, a:b])):
+        send([part(off, name, v, [(T.cores[c], v) for c in same]), part(rest, name, v, [(rl, v), (pc, v)])], [off, rest])
+    g.sem_inc(sem.gate, 1)
+
+    wait("ve", "lw1", 16)
+    w1_ready = quant(T.w1c, T.w1p, 0, T.w1t, 0, 512)
+    order = same + [p] + opp + [r]
+    t_ready, t_ends = {}, {}
+
+    def first(c):
+        pos = order.index(c)
+        if c == r:
+            wait("te", "ve", x_ready)
+        else:
+            wait("te", "xa%d" % c, 8)
+            wait("te", "xb%d" % c, 8)
+        wait("te", "ve", w1_ready)
+        t_ready[pos], t_ends[pos] = layer(T.w1c, T.w1p, 0, T.xc, T.xp, 128 * c, T.tt, T.tc, T.tp, pos)
+
+    first(r)
+    wait("ve", "lw2", 16)
+    w2_ready = quant(T.w2c, T.w2p, 0, T.w2t, 0, 512)
+    wait("g", "ve", w2_ready)
+    send([part(rest, "w2s", _codes(T.w2c, 0, 512), [(pc, _codes(T.w2c, 512, 1024))])], [rest])
+    send([part(rest, "w2s", T.w2p[:, 0:512], [(pc, T.w2p[:, 512:1024])])], [rest])
+    first(p)
+    n_on, n_rest = bin(on).count("1"), bin(rest).count("1")
+    for c in same:
+        first(c)
+    for i, (lo, hi) in enumerate(((0, 1), (1, 4))):
+        for q in range(lo, hi):
+            wait("g", "ve", t_ready[q])
+        lo, hi = 128 * lo, 128 * hi
+        send([part(on, "ts%d" % i, _codes(T.tc, lo, hi), [(pc, _codes(T.rc, lo, hi))])], [on])
+        send([part(on, "ts%d" % i, T.tp[:, lo:hi], [(pc, T.rp[:, lo:hi])])], [on])
+    wait("ve", "lw3", 16)
+    wait("ve", "lw4", 16)
+    quant(T.w34c, T.w34p, 0, T.w3t, 0, 512)
+    w34_ready = quant(T.w34c, T.w34p, 512, T.w4t, 0, 128)
+
+    def sums(i):
+        wait("te", "ve", t_ready[4 + i] if i < 3 else t_ready[7])
+        wait("te", "w2s", 2 * n_rest)
+        wait("te", "ts%d" % min(i, 1), 2 * n_on)
+        return [product([(T.w2c, T.w2p, 128 * m, T.tc, T.tp, 128 * (4 + i)),
+                         (T.w2c, T.w2p, 512 + 128 * m, T.rc, T.rp, 128 * i)]) for m in range(4)]
+
+    for i, s in enumerate(steps):
+        first(opp[i])
+        res = sums(i)
+        ends = [empty("ac" if m % 2 == 0 else "ve", res[m], T.so[:, 512 * i + 128 * m:512 * i + 128 * m + 128])
+                for m in range(4)]
+        for e in ends:
+            wait("g", *e)
+        a, d = 512 * i, 512 * (s - 1)
+        send([part(off, "sd%d" % s, T.so[:, a:a + 256], [(T.cores[opp[i]], T.si[:, d:d + 256])]),
+              part(rest, "rs%d" % s, T.so[:, a + 256:a + 512], [(rl, T.rl[:, 256 * i:256 * i + 256])])],
+             [off, rest], "ssent")
+    wait("g", "ve", w34_ready)
+    send([part(rest, "w34s", _codes(T.w34c, 0, 640), [(pc, _codes(T.w34c, 640, 1280))])], [rest])
+    send([part(rest, "w34s", T.w34p[:, 0:640], [(pc, T.w34p[:, 640:1280])])], [rest])
+    own = sums(3)
+
+    last = [0] * 4
+    for i, s in enumerate(steps):
+        d = 512 * (s - 1)
+        for h, name in ((0, "sd%d" % s), (1, "sh%d" % s)):
+            wait("ve", name, 8)
+            if i == 0:
+                for m in (2 * h, 2 * h + 1):
+                    b, cnt = own[m]
+                    wait("ve", "te", cnt)
+                    last[m] = done(ve.tensor_tensor(T.sacc[:, 128 * m:128 * m + 128], banks[b][:, 0:128],
+                                                    T.si[:, d + 128 * m:d + 128 * m + 128], ADD), "ve")
+                    free[b] = ("ve", last[m])
+            else:
+                lo, hi = 256 * h, 256 * h + 256
+                wait("ve", "ve", last[2 * h + 1])
+                last[2 * h] = last[2 * h + 1] = done(ve.tensor_tensor(T.sacc[:, lo:hi], T.sacc[:, lo:hi],
+                                                                      T.si[:, d + lo:d + hi], ADD), "ve")
+    h_ends = []
+    for m in range(4):
+        out, src = T.ht[:, m:512:4], T.sacc[:, 128 * m:128 * m + 128]
+        if m < 3:
+            wait("ac", "ve", last[m])
+            h_ends.append(("ac", done(ac.activation(out, src, RELU, scale=C2), "ac")))
+        else:
+            wait("ve", "ve", last[m])
+            h_ends.append(("ve", done(ve.tensor_scalar(out, src, 0.0, C2, MAX, MUL), "ve")))
+    for e in h_ends:
+        wait("ve", *e)
+    h_ready = quant(T.hc, T.hp, 0, T.ht, 0, 128)
+    wait("g", "ve", h_ready)
+    send([part(off, "hs%d" % k, _codes(T.hc, 0, 128),
+               [(T.cores[c], _codes(T.hc, 128 * s, 128 * s + 128)) for s, c in zip(steps, same)])], [off], "hsent")
+    send([part(off, "hs%d" % k, T.hp[:, 0:128],
+               [(T.cores[c], T.hp[:, 128 * s:128 * s + 128]) for s, c in zip(steps, same)])], [off], "hsent")
+
+    def store(c):
+        pos = order.index(c)
+        for e in t_ends[pos]:
+            wait("sy", *e)
+        sy.dma_start(T.t[c], T.tt[:, 512 * pos:512 * pos + 512]).then_inc(sem.st, 16)
+
+    wait("sy", "ssent", local["ssent"])
+    for c in order[:4]:
+        store(c)
+    wait("sy", "hsent", local["hsent"])
+    for c in order[4:]:
+        store(c)
+    for e in h_ends:
+        wait("sy", *e)
+    sy.dma_start(T.h[:], T.ht[:]).then_inc(sem.st, 16)
+
+    u_ready = {}
+
+    def second(s, w):
+        if s == 0:
+            wait("te", "ve", h_ready)
+        else:
+            wait("te", "hs%d" % (k ^ s), 16)
+        wait("te", "ve", w34_ready)
+        if w:
+            wait("te", "w34s", 2 * n_rest)
+        pos = 2 * s + w
+        u_ready[pos] = layer(T.w34c, T.w34p, 640 * w, T.hc, T.hp, 128 * s, T.ut, T.uc, T.up, pos)[0]
+
+    y_last = [0]
+
+    def third(s):
+        for w in (0, 1):
+            wait("te", "ve", u_ready[2 * s + w])
+        res = product([(T.w34c, T.w34p, 640 * w + 512, T.uc, T.up, 128 * (2 * s + w)) for w in (0, 1)])
+        if s == 0:
+            y_last[0] = empty("ve", res, T.ya[:])[1]
+            return
+        e = empty("ac", res, T.yo[:, 128 * (s - 1):128 * s])
+        wait("g", *e)
+        send([part(off, "ys%d" % s, T.yo[:, 128 * (s - 1):128 * s],
+                   [(T.cores[same[steps.index(s)]], T.yi[:, 128 * (s - 1):128 * s])])], [off])
+
+    second(0, 0)
+    second(0, 1)
+    third(0)
+    second(steps[0], 0)
+    second(steps[0], 1)
+    second(steps[1], 0)
+    third(steps[0])
+    second(steps[1], 1)
+    second(steps[2], 0)
+    third(steps[1])
+    second(steps[2], 1)
+    third(steps[2])
+    for s in steps:
+        wait("ve", "ys%d" % s, 8)
+        wait("ve", "ve", y_last[0])
+        y_last[0] = done(ve.tensor_tensor(T.ya[:], T.ya[:], T.yi[:, 128 * (s - 1):128 * s], ADD), "ve")
+    wait("sy", "ve", y_last[0])
+    sy.dma_start(T.y[:], T.ya[:]).then_inc(sem.st, 16)
+    wait("sy", "st", 16 * 10)
+    wait("g", "sent", local["sent"])
+    for q in ("te", "ve", "ac"):
+        wait("g", q, n[q])

@@ -22,10 +22,11 @@ for _b in range(8):
     SCRATCH["z%d" % _b] = ("psum", [128, 512], F32)
 SEMAPHORES = (["xa%d" % c for c in range(8)] + ["xb%d" % c for c in range(8)] + ["w2s", "w34s", "ts0", "ts1"]
               + ["%s%d" % (n, s) for n in ("sd", "sh", "rs", "ys") for s in (1, 2, 3)] + ["hs%d" % k for k in range(4)]
-              + ["lx", "lw1", "lw2", "lw3", "lw4", "st", "te", "ve", "ac", "gate", "sent", "ssent", "hsent"])
+              + ["lx", "lw1", "lw2", "lw3", "lw4", "st", "te", "ve", "ac", "xsent", "sent", "ssent", "hsent"])
 C1, C2 = float(np.float32(0.043)), float(np.float32(0.0152))
 ADD, MAX, MUL = AluOpType.add, AluOpType.max, AluOpType.mult
 RELU, COPY = ActivationFunctionType.Relu, ActivationFunctionType.Copy
+FIRST_THEN_REST = ((0,), (1, 2))
 
 
 def _layout(T, topo):
@@ -74,14 +75,16 @@ def _relay(g, T, topo, core, r, opp):
     wait, part, send, local = _tools(g, T, topo)
     a, b = 128 * r, 128 * r + 128
     off = topo.mask(core, opp[0][1])
-    wait("g", "xa%d" % r, 8)
-    send([part(off, "xa%d" % r, _codes(T.xc, a, b), [(c, _codes(T.xc, a, b)) for _, c in opp])], [off])
-    wait("g", "xb%d" % r, 8)
-    send([part(off, "xb%d" % r, T.xp[:, a:b], [(c, T.xp[:, a:b]) for _, c in opp])], [off])
+    for group in FIRST_THEN_REST:
+        to = [opp[i][1] for i in group]
+        wait("g", "xa%d" % r, 8)
+        send([part(off, "xa%d" % r, _codes(T.xc, a, b), [(c, _codes(T.xc, a, b)) for c in to])], [off])
+        wait("g", "xb%d" % r, 8)
+        send([part(off, "xb%d" % r, T.xp[:, a:b], [(c, T.xp[:, a:b]) for c in to])], [off])
     for i, (s, c) in enumerate(opp):
         wait("g", "rs%d" % s, 8)
         send([part(off, "sh%d" % s, T.rl[:, 256 * i:256 * i + 256],
-                   [(c, T.si[:, 512 * (s - 1) + 256:512 * s])])], [off])
+                   [(c, T.si[:, 512 * (s - 1):512 * (s - 1) + 256])])], [off])
     wait("g", "sent", local["sent"])
 
 
@@ -106,6 +109,7 @@ def rank_program(g, core, T, topo):
     sem = T.sem
     on, off = topo.mask(core, pc), topo.mask(core, T.cores[same[0]])
     rest = on & ~off
+    n_on, n_rest, n_off = (bin(m).count("1") for m in (on, rest, off))
     te, ve, ac, sy = g.tensor, g.vector, g.scalar, g.sync
     n = {"te": 0, "ve": 0, "ac": 0}
 
@@ -116,8 +120,8 @@ def rank_program(g, core, T, topo):
 
     sy.dma_start(T.xt[:], T.x[:]).then_inc(sem.lx, 16)
     sy.dma_start(T.w1t[:], T.w1[:]).then_inc(sem.lw1, 16)
-    wait("sy", "gate", 1)
     sy.dma_start(T.w2t[:], T.w2[:]).then_inc(sem.lw2, 16)
+    wait("sy", "xsent", 2 * (n_off + n_rest))
     sy.dma_start(T.w3t[:], T.w3[:]).then_inc(sem.lw3, 16)
     sy.dma_start(T.w4t[:], T.w4[:]).then_inc(sem.lw4, 16)
 
@@ -161,8 +165,8 @@ def rank_program(g, core, T, topo):
     a, b = 128 * r, 128 * r + 128
     wait("g", "ve", x_ready)
     for name, v in (("xa%d" % r, _codes(T.xc, a, b)), ("xb%d" % r, T.xp[:, a:b])):
-        send([part(off, name, v, [(T.cores[c], v) for c in same]), part(rest, name, v, [(rl, v), (pc, v)])], [off, rest])
-    g.sem_inc(sem.gate, 1)
+        send([part(off, name, v, [(T.cores[c], v) for c in same]), part(rest, name, v, [(rl, v), (pc, v)])],
+             [off, rest], "xsent")
 
     wait("ve", "lw1", 16)
     w1_ready = quant(T.w1c, T.w1p, 0, T.w1t, 0, 512)
@@ -186,7 +190,6 @@ def rank_program(g, core, T, topo):
     send([part(rest, "w2s", _codes(T.w2c, 0, 512), [(pc, _codes(T.w2c, 512, 1024))])], [rest])
     send([part(rest, "w2s", T.w2p[:, 0:512], [(pc, T.w2p[:, 512:1024])])], [rest])
     first(p)
-    n_on, n_rest = bin(on).count("1"), bin(rest).count("1")
     for c in same:
         first(c)
     for i, (lo, hi) in enumerate(((0, 1), (1, 4))):
@@ -195,29 +198,37 @@ def rank_program(g, core, T, topo):
         lo, hi = 128 * lo, 128 * hi
         send([part(on, "ts%d" % i, _codes(T.tc, lo, hi), [(pc, _codes(T.rc, lo, hi))])], [on])
         send([part(on, "ts%d" % i, T.tp[:, lo:hi], [(pc, T.rp[:, lo:hi])])], [on])
-    wait("ve", "lw3", 16)
-    wait("ve", "lw4", 16)
-    quant(T.w34c, T.w34p, 0, T.w3t, 0, 512)
-    w34_ready = quant(T.w34c, T.w34p, 512, T.w4t, 0, 128)
 
     def sums(i):
-        wait("te", "ve", t_ready[4 + i] if i < 3 else t_ready[7])
+        wait("te", "ve", t_ready[4 + i])
         wait("te", "w2s", 2 * n_rest)
         wait("te", "ts%d" % min(i, 1), 2 * n_on)
         return [product([(T.w2c, T.w2p, 128 * m, T.tc, T.tp, 128 * (4 + i)),
                          (T.w2c, T.w2p, 512 + 128 * m, T.rc, T.rp, 128 * i)]) for m in range(4)]
 
-    for i, s in enumerate(steps):
-        first(opp[i])
+    def send_sum(i):
+        s = steps[i]
         res = sums(i)
-        ends = [empty("ac" if m % 2 == 0 else "ve", res[m], T.so[:, 512 * i + 128 * m:512 * i + 128 * m + 128])
-                for m in range(4)]
-        for e in ends:
-            wait("g", *e)
         a, d = 512 * i, 512 * (s - 1)
-        send([part(off, "sd%d" % s, T.so[:, a:a + 256], [(T.cores[opp[i]], T.si[:, d:d + 256])]),
-              part(rest, "rs%d" % s, T.so[:, a + 256:a + 512], [(rl, T.rl[:, 256 * i:256 * i + 256])])],
-             [off, rest], "ssent")
+        ends = [empty("ac" if m % 2 == 0 else "ve", res[m], T.so[:, a + 128 * m:a + 128 * m + 128]) for m in range(4)]
+        for e in ends[:2]:
+            wait("g", *e)
+        send([part(rest, "rs%d" % s, T.so[:, a:a + 256], [(rl, T.rl[:, 256 * i:256 * i + 256])])], [rest], "ssent")
+        for e in ends[2:]:
+            wait("g", *e)
+        send([part(off, "sd%d" % s, T.so[:, a + 256:a + 512], [(T.cores[opp[i]], T.si[:, d + 256:d + 512])])],
+             [off], "ssent")
+
+    first(opp[0])
+    send_sum(0)
+    first(opp[1])
+    first(opp[2])
+    send_sum(1)
+    send_sum(2)
+    wait("ve", "lw3", 16)
+    wait("ve", "lw4", 16)
+    quant(T.w34c, T.w34p, 0, T.w3t, 0, 512)
+    w34_ready = quant(T.w34c, T.w34p, 512, T.w4t, 0, 128)
     wait("g", "ve", w34_ready)
     send([part(rest, "w34s", _codes(T.w34c, 0, 640), [(pc, _codes(T.w34c, 640, 1280))])], [rest])
     send([part(rest, "w34s", T.w34p[:, 0:640], [(pc, T.w34p[:, 640:1280])])], [rest])
@@ -226,24 +237,24 @@ def rank_program(g, core, T, topo):
     last = [0] * 4
     for i, s in enumerate(steps):
         d = 512 * (s - 1)
-        for h, name in ((0, "sd%d" % s), (1, "sh%d" % s)):
+        for ms, name in (((2, 3), "sd%d" % s), ((0, 1), "sh%d" % s)):
             wait("ve", name, 8)
             if i == 0:
-                for m in (2 * h, 2 * h + 1):
+                for m in ms:
                     b, cnt = own[m]
                     wait("ve", "te", cnt)
                     last[m] = done(ve.tensor_tensor(T.sacc[:, 128 * m:128 * m + 128], banks[b][:, 0:128],
                                                     T.si[:, d + 128 * m:d + 128 * m + 128], ADD), "ve")
                     free[b] = ("ve", last[m])
             else:
-                lo, hi = 256 * h, 256 * h + 256
-                wait("ve", "ve", last[2 * h + 1])
-                last[2 * h] = last[2 * h + 1] = done(ve.tensor_tensor(T.sacc[:, lo:hi], T.sacc[:, lo:hi],
-                                                                      T.si[:, d + lo:d + hi], ADD), "ve")
+                lo, hi = 128 * ms[0], 128 * ms[1] + 128
+                wait("ve", "ve", last[ms[1]])
+                v = done(ve.tensor_tensor(T.sacc[:, lo:hi], T.sacc[:, lo:hi], T.si[:, d + lo:d + hi], ADD), "ve")
+                last[ms[0]] = last[ms[1]] = v
     h_ends = []
-    for m in range(4):
+    for m in (2, 3, 0, 1):
         out, src = T.ht[:, m:512:4], T.sacc[:, 128 * m:128 * m + 128]
-        if m < 3:
+        if m != 1:
             wait("ac", "ve", last[m])
             h_ends.append(("ac", done(ac.activation(out, src, RELU, scale=C2), "ac")))
         else:
@@ -253,10 +264,10 @@ def rank_program(g, core, T, topo):
         wait("ve", *e)
     h_ready = quant(T.hc, T.hp, 0, T.ht, 0, 128)
     wait("g", "ve", h_ready)
-    send([part(off, "hs%d" % k, _codes(T.hc, 0, 128),
-               [(T.cores[c], _codes(T.hc, 128 * s, 128 * s + 128)) for s, c in zip(steps, same)])], [off], "hsent")
-    send([part(off, "hs%d" % k, T.hp[:, 0:128],
-               [(T.cores[c], T.hp[:, 128 * s:128 * s + 128]) for s, c in zip(steps, same)])], [off], "hsent")
+    for group in FIRST_THEN_REST:
+        to = [(T.cores[same[i]], 128 * steps[i]) for i in group]
+        send([part(off, "hs%d" % k, _codes(T.hc, 0, 128), [(c, _codes(T.hc, a, a + 128)) for c, a in to])], [off], "hsent")
+        send([part(off, "hs%d" % k, T.hp[:, 0:128], [(c, T.hp[:, a:a + 128]) for c, a in to])], [off], "hsent")
 
     def store(c):
         pos = order.index(c)

@@ -26,7 +26,6 @@ SEMAPHORES = (["xa%d" % c for c in range(8)] + ["xb%d" % c for c in range(8)] + 
 C1, C2 = float(np.float32(0.043)), float(np.float32(0.0152))
 ADD, MAX, MUL = AluOpType.add, AluOpType.max, AluOpType.mult
 RELU, COPY = ActivationFunctionType.Relu, ActivationFunctionType.Copy
-FIRST_THEN_REST = ((0,), (1, 2))
 
 
 def _layout(T, topo):
@@ -56,35 +55,34 @@ def _tools(g, T, topo):
         rid, pid, _ = topo.addr(c)
         return DstId(rid=rid, pnc=pid)
 
-    def part(mask, sem, src, outs):
-        return RemoteDMATransfer(dst_ids=[dest(c) for c, _ in outs], dma_engine_mask=mask, remote_sem=T.sem[sem],
-                                 srcs=[src], dsts=[o for _, o in outs])
+    def send(mask, name, src, outs, sem="sent"):
+        g.remote_dma_fused([RemoteDMATransfer(dst_ids=[dest(c) for c, _ in outs], dma_engine_mask=mask,
+                                              remote_sem=T.sem[name], srcs=[src], dsts=[o for _, o in outs])],
+                           local_sem=T.sem[sem])
+        local[sem] = local.get(sem, 0) + bin(mask).count("1")
 
-    def send(parts, masks, sem="sent"):
-        g.remote_dma_fused(parts, local_sem=T.sem[sem])
-        local[sem] = local.get(sem, 0) + sum(bin(m).count("1") for m in masks)
-
-    return wait, part, send, local
+    return wait, send, local
 
 
 def _codes(buf, a, b):
     return buf[:, a:b].bitcast(dt.uint8)
 
 
-def _relay(g, T, topo, core, r, opp):
-    wait, part, send, local = _tools(g, T, topo)
+def _relay(g, T, topo, core, r, n_first, opp, hname, hcol, hdst):
+    wait, send, local = _tools(g, T, topo)
     a, b = 128 * r, 128 * r + 128
     off = topo.mask(core, opp[0][1])
-    for group in FIRST_THEN_REST:
-        to = [opp[i][1] for i in group]
+    for s, c in opp:
         wait("g", "xa%d" % r, 8)
-        send([part(off, "xa%d" % r, _codes(T.xc, a, b), [(c, _codes(T.xc, a, b)) for c in to])], [off])
+        send(off, "xa%d" % r, _codes(T.xc, a, b), [(c, _codes(T.xc, a, b))])
         wait("g", "xb%d" % r, 8)
-        send([part(off, "xb%d" % r, T.xp[:, a:b], [(c, T.xp[:, a:b]) for c in to])], [off])
+        send(off, "xb%d" % r, T.xp[:, a:b], [(c, T.xp[:, a:b])])
     for i, (s, c) in enumerate(opp):
-        wait("g", "rs%d" % s, 8)
-        send([part(off, "sh%d" % s, T.rl[:, 256 * i:256 * i + 256],
-                   [(c, T.si[:, 512 * (s - 1):512 * (s - 1) + 256])])], [off])
+        wait("g", "rs%d" % s, n_first if i == 0 else 8)
+        send(off, "sh%d" % s, T.rl[:, 256 * i:256 * i + 256], [(c, T.si[:, 512 * (s - 1):512 * (s - 1) + 256])])
+    wait("g", hname, 16)
+    send(off, hname, _codes(T.hc, 0, 128), [(hdst, _codes(T.hc, hcol, hcol + 128))])
+    send(off, hname, T.hp[:, 0:128], [(hdst, T.hp[:, hcol:hcol + 128])])
     wait("g", "sent", local["sent"])
 
 
@@ -96,7 +94,10 @@ def rank_program(g, core, T, topo):
     steps = sorted((1, 2, 3), key=lambda s: (not topo.same_plane(chips[k], chips[k ^ s]), s))
     if core in relays[k]:
         j = relays[k].index(core)
-        return _relay(g, T, topo, core, ranks[k][j], [(s, T.cores[ranks[k ^ s][1 - j]]) for s in steps])
+        rc = T.cores[ranks[k][j]]
+        return _relay(g, T, topo, core, ranks[k][j], bin(topo.mask(rc, core)).count("1"),
+                      [(s, T.cores[ranks[k ^ s][1 - j]]) for s in steps],
+                      "hs%d" % k, 128 * steps[2], T.cores[ranks[k ^ steps[2]][j]])
     r = T.rank_of(core)
     if r is None:
         return
@@ -105,11 +106,11 @@ def rank_program(g, core, T, topo):
     pc, rl = T.cores[p], relays[k][j]
     same = [ranks[k ^ s][j] for s in steps]
     opp = [ranks[k ^ s][1 - j] for s in steps]
-    wait, part, send, local = _tools(g, T, topo)
+    wait, send, local = _tools(g, T, topo)
     sem = T.sem
     on, off = topo.mask(core, pc), topo.mask(core, T.cores[same[0]])
     rest = on & ~off
-    n_on, n_rest, n_off = (bin(m).count("1") for m in (on, rest, off))
+    n_on, n_rest = bin(on).count("1"), bin(rest).count("1")
     te, ve, ac, sy = g.tensor, g.vector, g.scalar, g.sync
     n = {"te": 0, "ve": 0, "ac": 0}
 
@@ -118,15 +119,28 @@ def rank_program(g, core, T, topo):
         n[q] += 1
         return n[q]
 
+    def quant(codes, plane, a, src, b, w):
+        return done(ve.quantize_mx(codes[:, a:a + w], plane[:, a:a + w], src[:, b:b + 4 * w]), "ve")
+
     sy.dma_start(T.xt[:], T.x[:]).then_inc(sem.lx, 16)
     sy.dma_start(T.w1t[:], T.w1[:]).then_inc(sem.lw1, 16)
     sy.dma_start(T.w2t[:], T.w2[:]).then_inc(sem.lw2, 16)
-    wait("sy", "xsent", 2 * (n_off + n_rest))
+    wait("ve", "lx", 16)
+    x_ready = quant(T.xc, T.xp, 128 * r, T.xt, 0, 128)
+    wait("g", "ve", x_ready)
+    a, b = 128 * r, 128 * r + 128
+    xs = (("xa%d" % r, _codes(T.xc, a, b)), ("xb%d" % r, T.xp[:, a:b]))
+    for name, v in xs:
+        send(off, name, v, [(T.cores[same[0]], v)], "xsent")
+        send(rest, name, v, [(rl, v)], "xsent")
+    for name, v in xs:
+        send(off, name, v, [(T.cores[c], v) for c in same[1:]], "xsent")
+    for name, v in xs:
+        send(rest, name, v, [(pc, v)], "xsent")
+
+    wait("sy", "xsent", local["xsent"])
     sy.dma_start(T.w3t[:], T.w3[:]).then_inc(sem.lw3, 16)
     sy.dma_start(T.w4t[:], T.w4[:]).then_inc(sem.lw4, 16)
-
-    def quant(codes, plane, a, src, b, w):
-        return done(ve.quantize_mx(codes[:, a:a + w], plane[:, a:a + w], src[:, b:b + 4 * w]), "ve")
 
     banks = [T["z%d" % b] for b in range(8)]
     free, turn = [None] * 8, [0]
@@ -160,14 +174,6 @@ def rank_program(g, core, T, topo):
             wait("ve", *e)
         return quant(codes, plane, 128 * pos, tile, 512 * pos, 128), ends
 
-    wait("ve", "lx", 16)
-    x_ready = quant(T.xc, T.xp, 128 * r, T.xt, 0, 128)
-    a, b = 128 * r, 128 * r + 128
-    wait("g", "ve", x_ready)
-    for name, v in (("xa%d" % r, _codes(T.xc, a, b)), ("xb%d" % r, T.xp[:, a:b])):
-        send([part(off, name, v, [(T.cores[c], v) for c in same]), part(rest, name, v, [(rl, v), (pc, v)])],
-             [off, rest], "xsent")
-
     wait("ve", "lw1", 16)
     w1_ready = quant(T.w1c, T.w1p, 0, T.w1t, 0, 512)
     order = same + [p] + opp + [r]
@@ -187,8 +193,8 @@ def rank_program(g, core, T, topo):
     wait("ve", "lw2", 16)
     w2_ready = quant(T.w2c, T.w2p, 0, T.w2t, 0, 512)
     wait("g", "ve", w2_ready)
-    send([part(rest, "w2s", _codes(T.w2c, 0, 512), [(pc, _codes(T.w2c, 512, 1024))])], [rest])
-    send([part(rest, "w2s", T.w2p[:, 0:512], [(pc, T.w2p[:, 512:1024])])], [rest])
+    send(rest, "w2s", _codes(T.w2c, 0, 512), [(pc, _codes(T.w2c, 512, 1024))])
+    send(rest, "w2s", T.w2p[:, 0:512], [(pc, T.w2p[:, 512:1024])])
     first(p)
     for c in same:
         first(c)
@@ -196,8 +202,8 @@ def rank_program(g, core, T, topo):
         for q in range(lo, hi):
             wait("g", "ve", t_ready[q])
         lo, hi = 128 * lo, 128 * hi
-        send([part(on, "ts%d" % i, _codes(T.tc, lo, hi), [(pc, _codes(T.rc, lo, hi))])], [on])
-        send([part(on, "ts%d" % i, T.tp[:, lo:hi], [(pc, T.rp[:, lo:hi])])], [on])
+        send(on, "ts%d" % i, _codes(T.tc, lo, hi), [(pc, _codes(T.rc, lo, hi))])
+        send(on, "ts%d" % i, T.tp[:, lo:hi], [(pc, T.rp[:, lo:hi])])
 
     def sums(i):
         wait("te", "ve", t_ready[4 + i])
@@ -213,15 +219,14 @@ def rank_program(g, core, T, topo):
         ends = [empty("ac" if m % 2 == 0 else "ve", res[m], T.so[:, a + 128 * m:a + 128 * m + 128]) for m in range(4)]
         for e in ends[:2]:
             wait("g", *e)
-        send([part(rest, "rs%d" % s, T.so[:, a:a + 256], [(rl, T.rl[:, 256 * i:256 * i + 256])])], [rest], "ssent")
+        send(on if i == 0 else rest, "rs%d" % s, T.so[:, a:a + 256], [(rl, T.rl[:, 256 * i:256 * i + 256])], "ssent")
         for e in ends[2:]:
             wait("g", *e)
-        send([part(off, "sd%d" % s, T.so[:, a + 256:a + 512], [(T.cores[opp[i]], T.si[:, d + 256:d + 512])])],
-             [off], "ssent")
+        send(off, "sd%d" % s, T.so[:, a + 256:a + 512], [(T.cores[opp[i]], T.si[:, d + 256:d + 512])], "ssent")
 
     first(opp[0])
-    send_sum(0)
     first(opp[1])
+    send_sum(0)
     first(opp[2])
     send_sum(1)
     send_sum(2)
@@ -230,8 +235,8 @@ def rank_program(g, core, T, topo):
     quant(T.w34c, T.w34p, 0, T.w3t, 0, 512)
     w34_ready = quant(T.w34c, T.w34p, 512, T.w4t, 0, 128)
     wait("g", "ve", w34_ready)
-    send([part(rest, "w34s", _codes(T.w34c, 0, 640), [(pc, _codes(T.w34c, 640, 1280))])], [rest])
-    send([part(rest, "w34s", T.w34p[:, 0:640], [(pc, T.w34p[:, 640:1280])])], [rest])
+    send(rest, "w34s", _codes(T.w34c, 0, 640), [(pc, _codes(T.w34c, 640, 1280))])
+    send(rest, "w34s", T.w34p[:, 0:640], [(pc, T.w34p[:, 640:1280])])
     own = sums(3)
 
     last = [0] * 4
@@ -264,10 +269,9 @@ def rank_program(g, core, T, topo):
         wait("ve", *e)
     h_ready = quant(T.hc, T.hp, 0, T.ht, 0, 128)
     wait("g", "ve", h_ready)
-    for group in FIRST_THEN_REST:
-        to = [(T.cores[same[i]], 128 * steps[i]) for i in group]
-        send([part(off, "hs%d" % k, _codes(T.hc, 0, 128), [(c, _codes(T.hc, a, a + 128)) for c, a in to])], [off], "hsent")
-        send([part(off, "hs%d" % k, T.hp[:, 0:128], [(c, T.hp[:, a:a + 128]) for c, a in to])], [off], "hsent")
+    for mask, c, a in ((off, T.cores[same[0]], 128 * steps[0]), (rest, rl, 0), (off, T.cores[same[1]], 128 * steps[1])):
+        send(mask, "hs%d" % k, _codes(T.hc, 0, 128), [(c, _codes(T.hc, a, a + 128))], "hsent")
+        send(mask, "hs%d" % k, T.hp[:, 0:128], [(c, T.hp[:, a:a + 128])], "hsent")
 
     def store(c):
         pos = order.index(c)
@@ -309,8 +313,8 @@ def rank_program(g, core, T, topo):
             return
         e = empty("ac", res, T.yo[:, 128 * (s - 1):128 * s])
         wait("g", *e)
-        send([part(off, "ys%d" % s, T.yo[:, 128 * (s - 1):128 * s],
-                   [(T.cores[same[steps.index(s)]], T.yi[:, 128 * (s - 1):128 * s])])], [off])
+        send(off, "ys%d" % s, T.yo[:, 128 * (s - 1):128 * s],
+             [(T.cores[same[steps.index(s)]], T.yi[:, 128 * (s - 1):128 * s])])
 
     second(0, 0)
     second(0, 1)
@@ -331,6 +335,7 @@ def rank_program(g, core, T, topo):
     wait("sy", "ve", y_last[0])
     sy.dma_start(T.y[:], T.ya[:]).then_inc(sem.st, 16)
     wait("sy", "st", 16 * 10)
-    wait("g", "sent", local["sent"])
+    for name in sorted(local):
+        wait("g", name, local[name])
     for q in ("te", "ve", "ac"):
         wait("g", q, n[q])

import numpy as np
from concourse.bass import DstId, RemoteDMATransfer
from concourse.mybir import dt, AluOpType, ActivationFunctionType

F8, U8, BF, F32 = "float8_e4m3fn_x4", "uint8", "bfloat16", "float32"
SCRATCH = {
    "xt": ("sbuf", [128, 512], BF), "w1t": ("sbuf", [128, 2048], BF), "w2t": ("sbuf", [128, 2048], BF),
    "w3t": ("sbuf", [128, 2048], BF), "w4t": ("sbuf", [128, 512], BF),
    "xc": ("sbuf", [128, 1024], F8), "xp": ("sbuf", [128, 1024], U8),
    "w1c": ("sbuf", [128, 512], F8), "w1p": ("sbuf", [128, 512], U8),
    "w2c": ("sbuf", [128, 1024], F8), "w2p": ("sbuf", [128, 1024], U8),
    "w34c": ("sbuf", [128, 1280], F8), "w34p": ("sbuf", [128, 1280], U8),
    "tt": ("sbuf", [128, 4096], BF), "tc": ("sbuf", [128, 1024], F8), "tp": ("sbuf", [128, 1024], U8),
    "rc": ("sbuf", [128, 512], F8), "rp": ("sbuf", [128, 512], U8),
    "so": ("sbuf", [128, 1536], F32), "si": ("sbuf", [128, 1536], F32), "sacc": ("sbuf", [128, 512], F32),
    "ht": ("sbuf", [128, 512], BF), "hc": ("sbuf", [128, 512], F8), "hp": ("sbuf", [128, 512], U8),
    "ut": ("sbuf", [128, 4096], BF), "uc": ("sbuf", [128, 1024], F8), "up": ("sbuf", [128, 1024], U8),
    "yo": ("sbuf", [128, 384], F32), "yi": ("sbuf", [128, 384], F32), "ya": ("sbuf", [128, 128], F32),
    "rl": ("sbuf", [128, 768], F32),
}
for _b in range(8):
    SCRATCH["z%d" % _b] = ("psum", [128, 512], F32)
SEMAPHORES = (["xa%d" % c for c in range(8)] + ["xb%d" % c for c in range(8)] + ["w2s", "w34s", "ts0", "ts1"]
              + ["%s%d" % (n, s) for n in ("sd", "sh", "rs", "ys") for s in (1, 2, 3)] + ["hs%d" % k for k in range(4)]
              + ["lx", "lw1", "lw2", "lw3", "lw4", "st", "te", "ve", "ac", "xsent", "sent", "ssent", "hsent"])
C1, C2 = float(np.float32(0.043)), float(np.float32(0.0152))
ADD, MAX, MUL = AluOpType.add, AluOpType.max, AluOpType.mult
RELU, COPY = ActivationFunctionType.Relu, ActivationFunctionType.Copy


def _layout(T, topo):
    chips = []
    for c in T.cores:
        if topo.chip(c) not in chips:
            chips.append(topo.chip(c))
    ranks = [[r for r, c in enumerate(T.cores) if topo.chip(c) == ch] for ch in chips]
    relays = []
    for ch, rs in zip(chips, ranks):
        own = T.cores[rs[0]]
        near = [c for c in range(128) if topo.chip(c) == ch and topo.die(c) != topo.die(own)]
        relays.append([c for c in near if all(topo.may_write(c, d) for d in T.cores)][:len(rs)])
    return chips, ranks, relays


def _tools(g, T, topo):
    queues = {"g": g, "te": g.tensor, "ve": g.vector, "ac": g.scalar, "sy": g.sync}
    seen, local = {}, {}

    def wait(q, sem, n):
        if n > seen.get((q, sem), 0):
            seen[(q, sem)] = n
            queues[q].wait_ge(T.sem[sem], n)

    def dest(c):
        rid, pid, _ = topo.addr(c)
        return DstId(rid=rid, pnc=pid)

    def send(mask, name, src, outs, sem="sent"):
        g.remote_dma_fused([RemoteDMATransfer(dst_ids=[dest(c) for c, _ in outs], dma_engine_mask=mask,
                                              remote_sem=T.sem[name], srcs=[src], dsts=[o for _, o in outs])],
                           local_sem=T.sem[sem])
        local[sem] = local.get(sem, 0) + bin(mask).count("1")

    return wait, send, local


def _codes(buf, a, b):
    return buf[:, a:b].bitcast(dt.uint8)


def _relay(g, T, topo, core, r, n_first, opp, hname, hcol, hdst):
    wait, send, local = _tools(g, T, topo)
    a, b = 128 * r, 128 * r + 128
    off = topo.mask(core, opp[0][1])
    for s, c in opp:
        wait("g", "xa%d" % r, 8)
        send(off, "xa%d" % r, _codes(T.xc, a, b), [(c, _codes(T.xc, a, b))])
        wait("g", "xb%d" % r, 8)
        send(off, "xb%d" % r, T.xp[:, a:b], [(c, T.xp[:, a:b])])
    for i, (s, c) in enumerate(opp):
        wait("g", "rs%d" % s, n_first if i == 0 else 8)
        send(off, "sh%d" % s, T.rl[:, 256 * i:256 * i + 256], [(c, T.si[:, 512 * (s - 1):512 * (s - 1) + 256])])
    wait("g", hname, 16)
    send(off, hname, _codes(T.hc, 0, 128), [(hdst, _codes(T.hc, hcol, hcol + 128))])
    send(off, hname, T.hp[:, 0:128], [(hdst, T.hp[:, hcol:hcol + 128])])
    wait("g", "sent", local["sent"])


def rank_program(g, core, T, topo):
    chips, ranks, relays = _layout(T, topo)
    if topo.chip(core) not in chips:
        return
    k = chips.index(topo.chip(core))
    steps = sorted((1, 2, 3), key=lambda s: (not topo.same_plane(chips[k], chips[k ^ s]), s))
    if core in relays[k]:
        j = relays[k].index(core)
        rc = T.cores[ranks[k][j]]
        return _relay(g, T, topo, core, ranks[k][j], bin(topo.mask(rc, core)).count("1"),
                      [(s, T.cores[ranks[k ^ s][1 - j]]) for s in steps],
                      "hs%d" % k, 128 * steps[2], T.cores[ranks[k ^ steps[2]][j]])
    r = T.rank_of(core)
    if r is None:
        return
    j = ranks[k].index(r)
    p = ranks[k][1 - j]
    pc, rl = T.cores[p], relays[k][j]
    same = [ranks[k ^ s][j] for s in steps]
    opp = [ranks[k ^ s][1 - j] for s in steps]
    wait, send, local = _tools(g, T, topo)
    sem = T.sem
    on, off = topo.mask(core, pc), topo.mask(core, T.cores[same[0]])
    rest = on & ~off
    n_on, n_rest = bin(on).count("1"), bin(rest).count("1")
    te, ve, ac, sy = g.tensor, g.vector, g.scalar, g.sync
    n = {"te": 0, "ve": 0, "ac": 0}

    def done(call, q):
        call.then_inc(sem[q], 1)
        n[q] += 1
        return n[q]

    def quant(codes, plane, a, src, b, w):
        return done(ve.quantize_mx(codes[:, a:a + w], plane[:, a:a + w], src[:, b:b + 4 * w]), "ve")

    sy.dma_start(T.xt[:], T.x[:]).then_inc(sem.lx, 16)
    sy.dma_start(T.w1t[:], T.w1[:]).then_inc(sem.lw1, 16)
    sy.dma_start(T.w2t[:], T.w2[:]).then_inc(sem.lw2, 16)
    wait("ve", "lx", 16)
    x_ready = quant(T.xc, T.xp, 128 * r, T.xt, 0, 128)
    wait("g", "ve", x_ready)
    a, b = 128 * r, 128 * r + 128
    xs = (("xa%d" % r, _codes(T.xc, a, b)), ("xb%d" % r, T.xp[:, a:b]))
    for name, v in xs:
        send(off, name, v, [(T.cores[same[0]], v)], "xsent")
        send(rest, name, v, [(rl, v)], "xsent")
    for name, v in xs:
        send(off, name, v, [(T.cores[c], v) for c in same[1:]], "xsent")
    for name, v in xs:
        send(rest, name, v, [(pc, v)], "xsent")

    wait("sy", "xsent", local["xsent"])
    sy.dma_start(T.w3t[:], T.w3[:]).then_inc(sem.lw3, 16)
    sy.dma_start(T.w4t[:], T.w4[:]).then_inc(sem.lw4, 16)

    banks = [T["z%d" % b] for b in range(8)]
    free, turn = [None] * 8, [0]

    def product(terms):
        b = turn[0]
        turn[0] = (b + 1) % 8
        if free[b]:
            wait("te", *free[b])
        for i, (wc, wp, a, xc, xp, c) in enumerate(terms):
            call = te.matmul_mx(banks[b][:, 0:128], wc[:, a:a + 128], wp[:, a:a + 128], xc[:, c:c + 128],
                                xp[:, c:c + 128], i == 0, i == len(terms) - 1)
        return b, done(call, "te")

    def empty(q, res, out, scale=None):
        b, m = res
        wait(q, "te", m)
        z = banks[b][:, 0:128]
        if q == "ac":
            call = ac.activation(out, z, COPY) if scale is None else ac.activation(out, z, RELU, scale=scale)
        else:
            call = ve.tensor_copy(out, z) if scale is None else ve.tensor_scalar(out, z, 0.0, scale, MAX, MUL)
        free[b] = (q, done(call, q))
        return free[b]

    def layer(wc, wp, a, xc, xp, c, tile, codes, plane, pos):
        res = [product([(wc, wp, a + 128 * i, xc, xp, c)]) for i in range(4)]
        ends = [empty("ac" if i % 2 == 0 else "ve", res[i], tile[:, 512 * pos + i:512 * pos + 512:4], C1)
                for i in range(4)]
        for e in ends[2:]:
            wait("ve", *e)
        return quant(codes, plane, 128 * pos, tile, 512 * pos, 128), ends

    wait("ve", "lw1", 16)
    w1_ready = quant(T.w1c, T.w1p, 0, T.w1t, 0, 512)
    order = same + [p] + opp + [r]
    t_ready, t_ends = {}, {}

    def first(c):
        pos = order.index(c)
        if c == r:
            wait("te", "ve", x_ready)
        else:
            wait("te", "xa%d" % c, 8)
            wait("te", "xb%d" % c, 8)
        wait("te", "ve", w1_ready)
        t_ready[pos], t_ends[pos] = layer(T.w1c, T.w1p, 0, T.xc, T.xp, 128 * c, T.tt, T.tc, T.tp, pos)

    first(r)
    wait("ve", "lw2", 16)
    w2_ready = quant(T.w2c, T.w2p, 0, T.w2t, 0, 512)
    wait("g", "ve", w2_ready)
    send(rest, "w2s", _codes(T.w2c, 0, 512), [(pc, _codes(T.w2c, 512, 1024))])
    send(rest, "w2s", T.w2p[:, 0:512], [(pc, T.w2p[:, 512:1024])])
    first(p)
    for c in same:
        first(c)
    for i, (lo, hi) in enumerate(((0, 1), (1, 4))):
        for q in range(lo, hi):
            wait("g", "ve", t_ready[q])
        lo, hi = 128 * lo, 128 * hi
        send(on, "ts%d" % i, _codes(T.tc, lo, hi), [(pc, _codes(T.rc, lo, hi))])
        send(on, "ts%d" % i, T.tp[:, lo:hi], [(pc, T.rp[:, lo:hi])])

    def sums(i):
        wait("te", "ve", t_ready[4 + i])
        wait("te", "w2s", 2 * n_rest)
        wait("te", "ts%d" % min(i, 1), 2 * n_on)
        return [product([(T.w2c, T.w2p, 128 * m, T.tc, T.tp, 128 * (4 + i)),
                         (T.w2c, T.w2p, 512 + 128 * m, T.rc, T.rp, 128 * i)]) for m in range(4)]

    def send_sum(i):
        s = steps[i]
        res = sums(i)
        a, d = 512 * i, 512 * (s - 1)
        ends = [empty("ac" if m % 2 == 0 else "ve", res[m], T.so[:, a + 128 * m:a + 128 * m + 128]) for m in range(4)]
        for e in ends[:2]:
            wait("g", *e)
        send(on if i == 0 else rest, "rs%d" % s, T.so[:, a:a + 256], [(rl, T.rl[:, 256 * i:256 * i + 256])], "ssent")
        for e in ends[2:]:
            wait("g", *e)
        send(off, "sd%d" % s, T.so[:, a + 256:a + 512], [(T.cores[opp[i]], T.si[:, d + 256:d + 512])], "ssent")

    first(opp[0])
    first(opp[1])
    send_sum(0)
    first(opp[2])
    send_sum(1)
    send_sum(2)
    wait("ve", "lw3", 16)
    wait("ve", "lw4", 16)
    quant(T.w34c, T.w34p, 0, T.w3t, 0, 512)
    w34_ready = quant(T.w34c, T.w34p, 512, T.w4t, 0, 128)
    wait("g", "ve", w34_ready)
    send(rest, "w34s", _codes(T.w34c, 0, 640), [(pc, _codes(T.w34c, 640, 1280))])
    send(rest, "w34s", T.w34p[:, 0:640], [(pc, T.w34p[:, 640:1280])])
    own = sums(3)

    last = [0] * 4
    for i, s in enumerate(steps):
        d = 512 * (s - 1)
        for ms, name in (((2, 3), "sd%d" % s), ((0, 1), "sh%d" % s)):
            wait("ve", name, 8)
            if i == 0:
                for m in ms:
                    b, cnt = own[m]
                    wait("ve", "te", cnt)
                    last[m] = done(ve.tensor_tensor(T.sacc[:, 128 * m:128 * m + 128], banks[b][:, 0:128],
                                                    T.si[:, d + 128 * m:d + 128 * m + 128], ADD), "ve")
                    free[b] = ("ve", last[m])
            else:
                lo, hi = 128 * ms[0], 128 * ms[1] + 128
                wait("ve", "ve", last[ms[1]])
                v = done(ve.tensor_tensor(T.sacc[:, lo:hi], T.sacc[:, lo:hi], T.si[:, d + lo:d + hi], ADD), "ve")
                last[ms[0]] = last[ms[1]] = v
    h_ends = []
    for m in (2, 3, 0, 1):
        out, src = T.ht[:, m:512:4], T.sacc[:, 128 * m:128 * m + 128]
        if m != 1:
            wait("ac", "ve", last[m])
            h_ends.append(("ac", done(ac.activation(out, src, RELU, scale=C2), "ac")))
        else:
            wait("ve", "ve", last[m])
            h_ends.append(("ve", done(ve.tensor_scalar(out, src, 0.0, C2, MAX, MUL), "ve")))
    for e in h_ends:
        wait("ve", *e)
    h_ready = quant(T.hc, T.hp, 0, T.ht, 0, 128)
    wait("g", "ve", h_ready)
    for mask, c, a in ((off, T.cores[same[0]], 128 * steps[0]), (rest, rl, 0), (off, T.cores[same[1]], 128 * steps[1])):
        send(mask, "hs%d" % k, _codes(T.hc, 0, 128), [(c, _codes(T.hc, a, a + 128))], "hsent")
        send(mask, "hs%d" % k, T.hp[:, 0:128], [(c, T.hp[:, a:a + 128])], "hsent")

    def store(c):
        pos = order.index(c)
        for e in t_ends[pos]:
            wait("sy", *e)
        sy.dma_start(T.t[c], T.tt[:, 512 * pos:512 * pos + 512]).then_inc(sem.st, 16)

    wait("sy", "ssent", local["ssent"])
    for c in order[:4]:
        store(c)
    wait("sy", "hsent", local["hsent"])
    for c in order[4:]:
        store(c)
    for e in h_ends:
        wait("sy", *e)
    sy.dma_start(T.h[:], T.ht[:]).then_inc(sem.st, 16)

    u_ready = {}

    def second(s, w):
        if s == 0:
            wait("te", "ve", h_ready)
        else:
            wait("te", "hs%d" % (k ^ s), 16)
        wait("te", "ve", w34_ready)
        if w:
            wait("te", "w34s", 2 * n_rest)
        pos = 2 * s + w
        u_ready[pos] = layer(T.w34c, T.w34p, 640 * w, T.hc, T.hp, 128 * s, T.ut, T.uc, T.up, pos)[0]

    y_last = [0]

    def third(s):
        for w in (0, 1):
            wait("te", "ve", u_ready[2 * s + w])
        res = product([(T.w34c, T.w34p, 640 * w + 512, T.uc, T.up, 128 * (2 * s + w)) for w in (0, 1)])
        if s == 0:
            y_last[0] = empty("ve", res, T.ya[:])[1]
            return
        e = empty("ac", res, T.yo[:, 128 * (s - 1):128 * s])
        wait("g", *e)
        send(off, "ys%d" % s, T.yo[:, 128 * (s - 1):128 * s],
             [(T.cores[same[steps.index(s)]], T.yi[:, 128 * (s - 1):128 * s])])

    second(0, 0)
    second(0, 1)
    third(0)
    second(steps[0], 0)
    second(steps[0], 1)
    second(steps[1], 0)
    third(steps[0])
    second(steps[1], 1)
    second(steps[2], 0)
    third(steps[1])
    second(steps[2], 1)
    third(steps[2])
    for s in steps:
        wait("ve", "ys%d" % s, 8)
        wait("ve", "ve", y_last[0])
        y_last[0] = done(ve.tensor_tensor(T.ya[:], T.ya[:], T.yi[:, 128 * (s - 1):128 * s], ADD), "ve")
    wait("sy", "ve", y_last[0])
    sy.dma_start(T.y[:], T.ya[:]).then_inc(sem.st, 16)
    wait("sy", "st", 16 * 10)
    for name in sorted(local):
        wait("g", name, local[name])
    for q in ("te", "ve", "ac"):
        wait("g", q, n[q])
